import numpy as np
import ml_dtypes


def mxq(x, axis, fmt="e4m3"):
    dtype, down = {"e4m3": (ml_dtypes.float8_e4m3fn, 7), "e5m2": (ml_dtypes.float8_e5m2, 14)}[fmt]
    v = np.moveaxis(np.asarray(x, np.float32).astype(ml_dtypes.bfloat16).astype(np.float64), axis, -1)
    blocks = v.reshape(v.shape[:-1] + (-1, 32))
    amax = np.abs(blocks).max(-1, keepdims=True)
    byte = np.maximum(np.where(amax > 0, np.frexp(amax)[1] - 1 + 127, 0) - down, 1)
    scale = np.exp2(byte - 127.0)
    codes = (blocks / scale).astype(np.float32).astype(dtype).astype(np.float64)
    return np.moveaxis((codes * scale).reshape(v.shape), -1, axis)


WIDE = False


def mx_kscale(k):
    if not WIDE:
        return np.ones(k)
    levels = np.array([10, -10, 5, -5, 0])
    if k % 512:
        return np.exp2(np.random.permutation(np.resize(levels, k // 32))).repeat(32)
    a = np.empty((k // 512, 16))
    for p in range(k // 512):
        a[p, :8] = np.random.permutation(np.resize(levels, 8))
        for g in range(8):
            far = levels[np.abs(levels - a[p, g]) >= 10]
            a[p, g + 8] = far[np.random.randint(len(far))]
    return np.exp2(a.ravel()).repeat(32)


def f64(x):
    return np.asarray(x).astype(np.float64)


def striped(idx):
    return np.tile(idx.reshape(-1, 16).T, (8, 1)).astype(np.uint16)


def unstriped(offs):
    return offs[:16].T.reshape(-1).astype(np.int64)


def pack_weight(w):
    k, n = w.shape
    w = f64(np.asarray(w, np.float32).astype(ml_dtypes.bfloat16)).reshape(k // 32, 32, n)
    amax = np.abs(w).max(1)
    byte = np.clip(np.where(amax > 0, np.frexp(amax)[1] - 1 + 127 - 7, 1), 1, 254)
    scaled = (w * np.exp2(127.0 - byte)[:, None, :]).reshape(k, n).astype(np.float32)
    words = np.ascontiguousarray(scaled.reshape(k // 512, 128, 4, n).transpose(0, 1, 3, 2)).astype(ml_dtypes.float8_e4m3fn).view(np.uint8)
    return words, np.ascontiguousarray(byte.astype(np.uint8).reshape(k // 512, 16, n))


def unpack_weight(words, scales):
    g, p, n, _ = words.shape
    vals = np.ascontiguousarray(words).view(ml_dtypes.float8_e4m3fn).astype(np.float64) * np.repeat(np.exp2(scales.astype(np.float64) - 127.0), 8, axis=1)[..., None]
    return vals.transpose(0, 1, 3, 2).reshape(g * 512, n)


K, T, S, V, H, N = 512, 1024, 512, 256, 512, 128


def setup_inputs():
    n = np.random.standard_normal
    s = mx_kscale(K)[:, None]
    u = mx_kscale(H)
    near = np.random.permutation(S)
    packed_xT = pack_weight(n((K, T)) * s)
    return {
        "x_words": packed_xT[0],
        "x_scales": packed_xT[1],
        "w1": (n((K, H)) / np.sqrt(K) / s * u).astype(np.float32),
        "w2": (n((H, N)) / np.sqrt(H) / u[:, None]).astype(np.float32),
        "el": (np.random.uniform(0.0, 0.8, (H, 1)) * u[:, None]).astype(np.float32),
        "offs": striped(np.random.permutation(T)[:S]),
        "pos1": striped(near[:V]),
        "pos2": striped(near[V:]),
        "pos3": striped(np.random.permutation(S)[:V]),
    }


def reference(x_words, x_scales, w1, w2, el, offs, pos1, pos2, pos3):
    xq = unpack_weight(x_words, x_scales)[:, unstriped(offs)]
    h = mxq(f64(w1), 0, "e4m3").T @ xq
    g0 = h[:, unstriped(pos1)]
    g1 = h[:, unstriped(pos2)]
    g2 = h[:, unstriped(pos3)]
    up = np.maximum(np.maximum(g0, g1), g2) + f64(el)
    lo = np.minimum(np.minimum(g0, g1), g2)
    z = up + lo - (2.0 * g0)
    return mxq(f64(w2), 0, "e4m3").T @ mxq(z, 0, "e4m3")

@@ -1,0 +1,207 @@
+from contextlib import ExitStack
+
+import concourse.mybir as mybir
+from concourse.masks import make_identity
+
+K, T, S, V, H, N = 512, 1024, 512, 256, 512, 128
+FLOPS = 2 * K * H * S + 2 * H * N * V
+
+F32 = mybir.dt.float32
+BF16 = mybir.dt.bfloat16
+I32 = mybir.dt.int32
+U32 = mybir.dt.uint32
+U16 = mybir.dt.uint16
+U8 = mybir.dt.uint8
+FP8X4 = mybir.dt.float8_e4m3fn_x4
+ALU = mybir.AluOpType
+ACT = mybir.ActivationFunctionType
+
+P = 128
+PACK = 4
+TILES = H // P
+HALF = V // 2
+Q = P // 2
+
+
+def tile_picked_ymorph_lap_p_kernel(
+    tc, x_words, x_scales, w1, w2, el, offs, pos1, pos2, pos3, out
+):
+    nc = tc.nc
+    with ExitStack() as ctx:
+        keep = ctx.enter_context(tc.tile_pool(name="keep", bufs=1))
+        psum = ctx.enter_context(tc.psum_pool(name="psum", bufs=1))
+
+        offs_sb = keep.tile([P, S // 16], U16, name="offs_sb")
+        pos_sb = [keep.tile([P, V // 16], U16, name=f"pos{d}") for d in range(3)]
+        xw = keep.tile([P, T], U32, name="xw", align_bytes=64)
+        xs = keep.tile([P, T], U8, name="xs", align_bytes=64)
+        w1_raw = [keep.tile([P, PACK, H // 2], F32, name=f"w1_raw{c}") for c in range(2)]
+        el_sb = keep.tile([P, PACK], F32, name="el_sb")
+        ident = keep.tile([P, P], F32, name="ident")
+
+        nc.gpsimd.memset(xs[:].bitcast(I32), 0)
+        nc.sync.dma_start(offs_sb[:], offs)
+        nc.sync.dma_start(xw[:].bitcast(I32), x_words[0].rearrange("p n t -> p (n t)").bitcast(I32))
+        for q in range(4):
+            nc.sync.dma_start(
+                xs[32 * q : 32 * q + 4, :].bitcast(I32), x_scales[0, 4 * q : 4 * q + 4, :].bitcast(I32)
+            )
+        w1_v = w1.rearrange("(p j) c -> p j c", j=PACK)
+        for c in range(2):
+            nc.sync.dma_start(w1_raw[c][:], w1_v[:, :, c * (H // 2) : (c + 1) * (H // 2)])
+        for d, pos in enumerate((pos1, pos2, pos3)):
+            nc.sync.dma_start(pos_sb[d][:], pos)
+        nc.sync.dma_start(el_sb[:], el.rearrange("(p t) o -> p (t o)", t=PACK))
+        make_identity(nc, ident[:])
+
+        ehalf = keep.tile([P, 2, V], F32, name="ehalf")
+
+        xq_s = keep.tile([P, S], U8, name="xq_s", align_bytes=64)
+        xq_w = keep.tile([P, S], U32, name="xq_w", align_bytes=64)
+        nc.vector.tensor_copy(xq_w[:], xw[:].indirect(offs_sb[:]))
+        nc.vector.tensor_copy(xq_s[:], xs[:].indirect(offs_sb[:]))
+
+        def quantise(grouped, name):
+            codes = keep.tile([P, P], U32, name=name + "_codes", align_bytes=64)
+            scales = keep.tile([P, P], U8, name=name + "_scales", align_bytes=64)
+            nc.vector.quantize_mx(out=codes[:].bitcast(FP8X4), scales=scales[:], in_=grouped)
+            return codes, scales
+
+        def product(acc, lhs, codes, scales):
+            nc.tensor.matmul_mx(
+                out=acc,
+                lhsT=lhs[0][:].bitcast(FP8X4),
+                lhsT_scale=lhs[1][:],
+                rhs=codes.bitcast(FP8X4),
+                rhs_scale=scales,
+                start=True,
+                stop=True,
+            )
+
+        w1_cols = [raw[:].rearrange("p j (m t) -> p m t j", t=PACK) for raw in w1_raw]
+        w1_pair = [keep.tile([P, 2, Q, PACK], BF16, name=f"w1_pair{c}", align_bytes=64) for c in range(2)]
+        w1_slot = keep.tile([P, 2, P, PACK], BF16, name="w1_slot", align_bytes=64)
+        h = [keep.tile([P, S], F32, name=f"h{j}") for j in range(TILES)]
+
+        def hidden(j):
+            if j < 2:
+                dst = w1_pair[j][:].rearrange("p e m j -> p m e j")
+                nc.scalar.copy(dst, w1_cols[j][:, :, 0:2, :])
+                w1_q = quantise(w1_pair[j][:].rearrange("p e m j -> p (e m j)"), f"w1_{j}")
+            else:
+                if j == 2:
+                    for c in range(2):
+                        nc.scalar.copy(
+                            w1_slot[:, :, c * Q : (c + 1) * Q, :].rearrange("p e m j -> p m e j"),
+                            w1_cols[c][:, :, 2:4, :],
+                        )
+                w1_q = quantise(w1_slot[:, j - 2, :, :].rearrange("p m j -> p (m j)"), f"w1_{j}")
+            if j == 0:
+                for u in range(2):
+                    cols = slice(u * S // 2, (u + 1) * S // 2)
+                    acc = psum.tile([P, S // 2], F32, name=f"narrow{u}")
+                    product(acc[:], w1_q, xq_w[:, cols], xq_s[:, cols])
+                    if u == 0:
+                        nc.scalar.copy(h[j][:, cols], acc[:])
+                    else:
+                        nc.vector.tensor_copy(h[j][:, cols], acc[:])
+            else:
+                acc = psum.tile([P, S], F32, name=f"h_acc{j}")
+                product(acc[:], w1_q, xq_w[:], xq_s[:])
+                nc.scalar.copy(h[j][:], acc[:])
+
+        base = [keep.tile([P, V], F32, name=f"base{j}") for j in range(TILES)]
+        da = [keep.tile([P, V], F32, name=f"da{j}") for j in range(TILES)]
+        db = [keep.tile([P, V], F32, name=f"db{j}") for j in range(TILES)]
+        up = [keep.tile([P, 2, V], F32, name=f"up{c}") for c in range(2)]
+        lo = [keep.tile([P, 2, V], F32, name=f"lo{c}") for c in range(2)]
+        zt = [psum.tile([P, 2, P], F32, name=f"zt{u}") for u in range(2)]
+        z_bf = [keep.tile([P, HALF, PACK], BF16, name=f"z_bf{u}", align_bytes=64) for u in range(2)]
+
+        def centre(j):
+            picked = h[j][:].indirect(pos_sb[0][:])
+            if j < 2:
+                nc.vector.tensor_copy(base[j][:], picked)
+            else:
+                nc.vector.tensor_tensor(base[j][:], picked, ehalf[:, j - 2, :], ALU.subtract)
+
+        def neighbour(j, d, dst):
+            nc.vector.tensor_tensor(dst[j][:], h[j][:].indirect(pos_sb[d][:]), base[j][:], ALU.subtract)
+
+        def extreme(j, dst, op):
+            own = 0.0 if j < 2 else ehalf[:, j - 2, 0:1]
+            nc.vector.scalar_tensor_tensor(dst[j // 2][:, j % 2, :], da[j][:], own, db[j][:], op, op)
+
+        def turn(dst, term, start, stop):
+            nc.tensor.matmul(dst, term, ident[:], start=start, stop=stop, is_transpose=True)
+
+        def turn_tile(j):
+            for src in (up, lo):
+                for u in range(2):
+                    cols = slice(u * HALF, (u + 1) * HALF)
+                    turn(zt[u][:, :, j * Q : (j + 1) * Q], src[0][:, j, cols], False, j == 1 and src is lo)
+
+        def turn_back():
+            back = psum.tile([P, 2, HALF], F32, name="back")
+            for u in range(2):
+                zt_bf = keep.tile([P, P, 2], BF16, name=f"zt_bf{u}")
+                nc.scalar.copy(zt_bf[:], zt[u][:].rearrange("v e p -> v p e"))
+                nc.tensor.transpose(back[:, u, :], zt_bf[:].rearrange("v p e -> v (p e)").bitcast(F32), ident[:])
+            for u in range(2):
+                words = z_bf[u][:].rearrange("p v t -> p (v t)").bitcast(F32).rearrange("p (v w) -> p v w", w=2)
+                nc.scalar.copy(words[:, :, 0], back[:, u, :])
+
+        hidden(0)
+        for j in range(TILES):
+            centre(j)
+            if j + 1 < TILES:
+                hidden(j + 1)
+            if j == 1:
+                nc.scalar.activation(
+                    ehalf[:], el_sb[:, 2:4].unsqueeze(2).to_broadcast([P, 2, V]), ACT.Copy, scale=0.5
+                )
+            if j == 0:
+                for u in range(2):
+                    for e in range(2):
+                        turn(zt[u][:, e, :], el_sb[:, e : e + 1].to_broadcast([P, HALF]), e == 0, False)
+            if j > 0:
+                extreme(j - 1, up, ALU.max)
+            neighbour(j, 1, da)
+            neighbour(j, 2, db)
+            if j > 0:
+                extreme(j - 1, lo, ALU.min)
+            if j in (1, 2):
+                turn_tile(j - 1)
+            if j == 2:
+                turn_back()
+                w2_raw = keep.tile([P, PACK, N], F32, name="w1_raw0")
+                nc.sync.dma_start(w2_raw[:], w2.rearrange("(p j) n -> p j n", j=PACK))
+                w2_bf = keep.tile([P, N, PACK], BF16, name="w2_bf", align_bytes=64)
+                nc.scalar.copy(
+                    w2_bf[:].rearrange("p (c i) j -> p c j i", i=4),
+                    w2_raw[:].rearrange("p j (c i) -> p c j i", i=4),
+                )
+                w2_q = quantise(w2_bf[:].rearrange("p n j -> p (n j)"), "w2")
+        extreme(TILES - 1, up, ALU.max)
+        extreme(TILES - 1, lo, ALU.min)
+
+        for u in range(2):
+            cols = slice(u * HALF, (u + 1) * HALF)
+            nc.vector.tensor_tensor(
+                z_bf[u][:, :, 2:4].rearrange("p (c i) t -> p c t i", i=4),
+                up[1][:, :, cols].rearrange("p t (c i) -> p c t i", i=4),
+                lo[1][:, :, cols].rearrange("p t (c i) -> p c t i", i=4),
+                ALU.add,
+            )
+        for u in range(2):
+            cols = slice(u * HALF, (u + 1) * HALF)
+            z_q = quantise(z_bf[u][:].rearrange("p v t -> p (v t)"), f"z{u}")
+            acc = psum.tile([P, HALF], F32, name=f"narrow{u}")
+            product(acc[:], w2_q, z_q[0][:], z_q[1][:])
+            res = keep.tile([P, HALF], F32, name=f"res{u}")
+            if u == 0:
+                nc.scalar.copy(res[:], acc[:])
+                nc.scalar.dma_start(out[:, cols], res[:])
+            else:
+                nc.vector.tensor_copy(res[:], acc[:])
+                nc.sync.dma_start(out[:, cols], res[:])

@@ -21,6 +21,8 @@ PACK = 4
 TILES = H // P
 HALF = V // 2
 Q = P // 2
+WHOLE = slice(0, V)
+HALVES = (slice(0, HALF), slice(HALF, V))
 
 
 def tile_picked_ymorph_lap_p_kernel(
@@ -35,7 +37,8 @@ def tile_picked_ymorph_lap_p_kernel(
         pos_sb = [keep.tile([P, V // 16], U16, name=f"pos{d}") for d in range(3)]
         xw = keep.tile([P, T], U32, name="xw", align_bytes=64)
         xs = keep.tile([P, T], U8, name="xs", align_bytes=64)
-        w1_raw = [keep.tile([P, PACK, H // 2], F32, name=f"w1_raw{c}") for c in range(2)]
+        w1_first = [keep.tile([P, 2, H // 2], F32, name=f"w1_first{r}") for r in range(2)]
+        w1_second = keep.tile([P, PACK, H // 2], F32, name="w1_second")
         el_sb = keep.tile([P, PACK], F32, name="el_sb")
         ident = keep.tile([P, P], F32, name="ident")
 
@@ -47,14 +50,15 @@ def tile_picked_ymorph_lap_p_kernel(
                 xs[32 * q : 32 * q + 4, :].bitcast(I32), x_scales[0, 4 * q : 4 * q + 4, :].bitcast(I32)
             )
         w1_v = w1.rearrange("(p j) c -> p j c", j=PACK)
-        for c in range(2):
-            nc.sync.dma_start(w1_raw[c][:], w1_v[:, :, c * (H // 2) : (c + 1) * (H // 2)])
+        for r in range(2):
+            nc.sync.dma_start(w1_first[r][:], w1_v[:, 2 * r : 2 * r + 2, 0 : H // 2])
+        nc.sync.dma_start(w1_second[:], w1_v[:, :, H // 2 : H])
         for d, pos in enumerate((pos1, pos2, pos3)):
             nc.sync.dma_start(pos_sb[d][:], pos)
         nc.sync.dma_start(el_sb[:], el.rearrange("(p t) o -> p (t o)", t=PACK))
         make_identity(nc, ident[:])
 
-        ehalf = keep.tile([P, 2, V], F32, name="ehalf")
+        el_half = keep.tile([P, 2], F32, name="el_half")
 
         xq_s = keep.tile([P, S], U8, name="xq_s", align_bytes=64)
         xq_w = keep.tile([P, S], U32, name="xq_w", align_bytes=64)
@@ -62,84 +66,102 @@ def tile_picked_ymorph_lap_p_kernel(
         nc.vector.tensor_copy(xq_s[:], xs[:].indirect(offs_sb[:]))
 
         def quantise(grouped, name):
-            codes = keep.tile([P, P], U32, name=name + "_codes", align_bytes=64)
-            scales = keep.tile([P, P], U8, name=name + "_scales", align_bytes=64)
+            width = grouped.shape[1] // PACK
+            codes = keep.tile([P, width], U32, name=name + "_codes", align_bytes=64)
+            scales = keep.tile([P, width], U8, name=name + "_scales", align_bytes=64)
             nc.vector.quantize_mx(out=codes[:].bitcast(FP8X4), scales=scales[:], in_=grouped)
-            return codes, scales
+            return codes[:], scales[:]
 
         def product(acc, lhs, codes, scales):
             nc.tensor.matmul_mx(
                 out=acc,
-                lhsT=lhs[0][:].bitcast(FP8X4),
-                lhsT_scale=lhs[1][:],
+                lhsT=lhs[0].bitcast(FP8X4),
+                lhsT_scale=lhs[1],
                 rhs=codes.bitcast(FP8X4),
                 rhs_scale=scales,
                 start=True,
                 stop=True,
             )
 
-        w1_cols = [raw[:].rearrange("p j (m t) -> p m t j", t=PACK) for raw in w1_raw]
+        first_cols = [raw[:].rearrange("p j (m t) -> p m t j", t=PACK) for raw in w1_first]
+        second_cols = w1_second[:].rearrange("p j (m t) -> p m t j", t=PACK)
         w1_pair = [keep.tile([P, 2, Q, PACK], BF16, name=f"w1_pair{c}", align_bytes=64) for c in range(2)]
         w1_slot = keep.tile([P, 2, P, PACK], BF16, name="w1_slot", align_bytes=64)
         h = [keep.tile([P, S], F32, name=f"h{j}") for j in range(TILES)]
 
+        h_lifted = [keep.tile([P, S], F32, name=f"h_lifted{e}") for e in range(2)]
+        extremes = []
+
+        for r in range(2):
+            nc.scalar.copy(
+                w1_pair[0][:, :, :, 2 * r : 2 * r + 2].rearrange("p e m j -> p m e j"), first_cols[r][:, :, 0:2, :]
+            )
+        w1_q = [quantise(w1_pair[0][:].rearrange("p e m j -> p (e m j)"), "w1_0")]
+        for u in range(2):
+            cols = slice(u * S // 2, (u + 1) * S // 2)
+            acc = psum.tile([P, S // 2], F32, name=f"narrow{u}")
+            product(acc[:], w1_q[0], xq_w[:, cols], xq_s[:, cols])
+            nc.vector.tensor_copy(h[0][:, cols], acc[:])
+
         def hidden(j):
-            if j < 2:
-                dst = w1_pair[j][:].rearrange("p e m j -> p m e j")
-                nc.scalar.copy(dst, w1_cols[j][:, :, 0:2, :])
-                w1_q = quantise(w1_pair[j][:].rearrange("p e m j -> p (e m j)"), f"w1_{j}")
-            else:
-                if j == 2:
-                    for c in range(2):
-                        nc.scalar.copy(
-                            w1_slot[:, :, c * Q : (c + 1) * Q, :].rearrange("p e m j -> p m e j"),
-                            w1_cols[c][:, :, 2:4, :],
-                        )
-                w1_q = quantise(w1_slot[:, j - 2, :, :].rearrange("p m j -> p (m j)"), f"w1_{j}")
-            if j == 0:
-                for u in range(2):
-                    cols = slice(u * S // 2, (u + 1) * S // 2)
-                    acc = psum.tile([P, S // 2], F32, name=f"narrow{u}")
-                    product(acc[:], w1_q, xq_w[:, cols], xq_s[:, cols])
-                    if u == 0:
-                        nc.scalar.copy(h[j][:, cols], acc[:])
-                    else:
-                        nc.vector.tensor_copy(h[j][:, cols], acc[:])
-            else:
-                acc = psum.tile([P, S], F32, name=f"h_acc{j}")
-                product(acc[:], w1_q, xq_w[:], xq_s[:])
-                nc.scalar.copy(h[j][:], acc[:])
+            if j == 1:
+                nc.scalar.copy(w1_pair[1][:].rearrange("p e m j -> p m e j"), second_cols[:, :, 0:2, :])
+                w1_q.append(quantise(w1_pair[1][:].rearrange("p e m j -> p (e m j)"), "w1_1"))
+            if j == 2:
+                nc.scalar.mul(el_half[:], el_sb[:, 2:4], 0.5)
+                for r in range(2):
+                    nc.scalar.copy(
+                        w1_slot[:, :, 0:Q, 2 * r : 2 * r + 2].rearrange("p e m j -> p m e j"),
+                        first_cols[r][:, :, 2:4, :],
+                    )
+                nc.scalar.copy(w1_slot[:, :, Q:P, :].rearrange("p e m j -> p m e j"), second_cols[:, :, 2:4, :])
+                codes, scales = quantise(w1_slot[:].rearrange("p e m j -> p (e m j)"), "w1_2")
+                for e in range(2):
+                    w1_q.append((codes[:, e * P : (e + 1) * P], scales[:, e * P : (e + 1) * P]))
+            acc = psum.tile([P, S], F32, name=f"h_acc{j}")
+            product(acc[:], w1_q[j], xq_w[:], xq_s[:])
+            nc.scalar.copy(h[j][:], acc[:])
+            if j >= 2:
+                lift = keep.tile([P, 1], F32, name=f"extremes{j - 2}")
+                nc.scalar.mul(lift[:], el_sb[:, j : j + 1], 0.5)
+                nc.scalar.activation(h_lifted[j - 2][:], acc[:], ACT.Identity, bias=lift[:])
+                extremes.append(keep.tile([P, 2, 2, V], F32, name=f"extremes{j - 2}"))
 
         base = [keep.tile([P, V], F32, name=f"base{j}") for j in range(TILES)]
-        da = [keep.tile([P, V], F32, name=f"da{j}") for j in range(TILES)]
-        db = [keep.tile([P, V], F32, name=f"db{j}") for j in range(TILES)]
-        up = [keep.tile([P, 2, V], F32, name=f"up{c}") for c in range(2)]
-        lo = [keep.tile([P, 2, V], F32, name=f"lo{c}") for c in range(2)]
+        da = [keep.tile([P, 2, V], F32, name=f"da{c}") for c in range(2)]
+        db = [keep.tile([P, 2, V], F32, name=f"db{c}") for c in range(2)]
         zt = [psum.tile([P, 2, P], F32, name=f"zt{u}") for u in range(2)]
         z_bf = [keep.tile([P, HALF, PACK], BF16, name=f"z_bf{u}", align_bytes=64) for u in range(2)]
 
-        def centre(j):
-            picked = h[j][:].indirect(pos_sb[0][:])
-            if j < 2:
-                nc.vector.tensor_copy(base[j][:], picked)
+        def centre(j, cols):
+            offsets = pos_sb[0][:, cols.start // 16 : cols.stop // 16]
+            nc.vector.tensor_copy(base[j][:, cols], h[j][:].indirect(offsets))
+
+        def neighbour(j, d, cols):
+            window = h[j] if j < 2 else h_lifted[j - 2]
+            offsets = pos_sb[d][:, cols.start // 16 : cols.stop // 16]
+            dst = (da, db)[d - 1][j // 2][:, j % 2, cols]
+            nc.vector.tensor_tensor(dst, window[:].indirect(offsets), base[j][:, cols], ALU.subtract)
+
+        def extreme(j, n, cols):
+            op = (ALU.max, ALU.min)[n]
+            if j == 1:
+                nc.vector.scalar_tensor_tensor(extremes[0][:, n, :, :], da[0][:], 0.0, db[0][:], op, op)
             else:
-                nc.vector.tensor_tensor(base[j][:], picked, ehalf[:, j - 2, :], ALU.subtract)
-
-        def neighbour(j, d, dst):
-            nc.vector.tensor_tensor(dst[j][:], h[j][:].indirect(pos_sb[d][:]), base[j][:], ALU.subtract)
-
-        def extreme(j, dst, op):
-            own = 0.0 if j < 2 else ehalf[:, j - 2, 0:1]
-            nc.vector.scalar_tensor_tensor(dst[j // 2][:, j % 2, :], da[j][:], own, db[j][:], op, op)
+                e = j - 2
+                nc.vector.scalar_tensor_tensor(
+                    extremes[1][:, n, e, cols], da[1][:, e, cols], el_half[:, e : e + 1], db[1][:, e, cols], op, op
+                )
 
         def turn(dst, term, start, stop):
             nc.tensor.matmul(dst, term, ident[:], start=start, stop=stop, is_transpose=True)
 
-        def turn_tile(j):
-            for src in (up, lo):
+        def turn_tile():
+            for n in range(2):
                 for u in range(2):
-                    cols = slice(u * HALF, (u + 1) * HALF)
-                    turn(zt[u][:, :, j * Q : (j + 1) * Q], src[0][:, j, cols], False, j == 1 and src is lo)
+                    for j in range(2):
+                        term = extremes[0][:, n, j, HALVES[u]]
+                        turn(zt[u][:, :, j * Q : (j + 1) * Q], term, False, j == 1 and n == 1)
 
         def turn_back():
             back = psum.tile([P, 2, HALF], F32, name="back")
@@ -151,53 +173,55 @@ def tile_picked_ymorph_lap_p_kernel(
                 words = z_bf[u][:].rearrange("p v t -> p (v t)").bitcast(F32).rearrange("p (v w) -> p v w", w=2)
                 nc.scalar.copy(words[:, :, 0], back[:, u, :])
 
-        hidden(0)
-        for j in range(TILES):
-            centre(j)
-            if j + 1 < TILES:
-                hidden(j + 1)
-            if j == 1:
-                nc.scalar.activation(
-                    ehalf[:], el_sb[:, 2:4].unsqueeze(2).to_broadcast([P, 2, V]), ACT.Copy, scale=0.5
-                )
-            if j == 0:
-                for u in range(2):
-                    for e in range(2):
-                        turn(zt[u][:, e, :], el_sb[:, e : e + 1].to_broadcast([P, HALF]), e == 0, False)
-            if j > 0:
-                extreme(j - 1, up, ALU.max)
-            neighbour(j, 1, da)
-            neighbour(j, 2, db)
-            if j > 0:
-                extreme(j - 1, lo, ALU.min)
-            if j in (1, 2):
-                turn_tile(j - 1)
-            if j == 2:
-                turn_back()
-                w2_raw = keep.tile([P, PACK, N], F32, name="w1_raw0")
-                nc.sync.dma_start(w2_raw[:], w2.rearrange("(p j) n -> p j n", j=PACK))
-                w2_bf = keep.tile([P, N, PACK], BF16, name="w2_bf", align_bytes=64)
-                nc.scalar.copy(
-                    w2_bf[:].rearrange("p (c i) j -> p c j i", i=4),
-                    w2_raw[:].rearrange("p j (c i) -> p c j i", i=4),
-                )
-                w2_q = quantise(w2_bf[:].rearrange("p n j -> p (n j)"), "w2")
-        extreme(TILES - 1, up, ALU.max)
-        extreme(TILES - 1, lo, ALU.min)
-
+        for j in range(2):
+            for cols in HALVES:
+                centre(j, cols)
+            hidden(j + 1)
+            neighbour(j, 1, HALVES[0])
+            neighbour(j, 2, WHOLE)
+            neighbour(j, 1, HALVES[1])
         for u in range(2):
-            cols = slice(u * HALF, (u + 1) * HALF)
+            for e in range(2):
+                turn(zt[u][:, e, :], el_sb[:, e : e + 1].to_broadcast([P, HALF]), e == 0, False)
+
+        centre(2, WHOLE)
+        hidden(3)
+        extreme(1, 0, WHOLE)
+        neighbour(2, 1, WHOLE)
+        extreme(1, 1, WHOLE)
+        neighbour(2, 2, WHOLE)
+        w2_raw = keep.tile([P, PACK, N], F32, name="w1_first0")
+        nc.sync.dma_start(w2_raw[:], w2.rearrange("(p j) n -> p j n", j=PACK))
+        w2_bf = keep.tile([P, N, PACK], BF16, name="w2_bf", align_bytes=64)
+        nc.scalar.copy(
+            w2_bf[:].rearrange("p (c i) j -> p c j i", i=4),
+            w2_raw[:].rearrange("p j (c i) -> p c j i", i=4),
+        )
+        w2_q = quantise(w2_bf[:].rearrange("p n j -> p (n j)"), "w2")
+        turn_tile()
+        turn_back()
+
+        centre(3, WHOLE)
+        extreme(2, 0, WHOLE)
+        neighbour(3, 1, WHOLE)
+        neighbour(3, 2, WHOLE)
+        extreme(2, 1, WHOLE)
+        extreme(3, 0, WHOLE)
+        for cols in HALVES:
+            extreme(3, 1, cols)
+
+        for u, cols in enumerate(HALVES):
             nc.vector.tensor_tensor(
                 z_bf[u][:, :, 2:4].rearrange("p (c i) t -> p c t i", i=4),
-                up[1][:, :, cols].rearrange("p t (c i) -> p c t i", i=4),
-                lo[1][:, :, cols].rearrange("p t (c i) -> p c t i", i=4),
+                extremes[1][:, 0, :, cols].rearrange("p t (c i) -> p c t i", i=4),
+                extremes[1][:, 1, :, cols].rearrange("p t (c i) -> p c t i", i=4),
                 ALU.add,
             )
         for u in range(2):
             cols = slice(u * HALF, (u + 1) * HALF)
             z_q = quantise(z_bf[u][:].rearrange("p v t -> p (v t)"), f"z{u}")
             acc = psum.tile([P, HALF], F32, name=f"narrow{u}")
-            product(acc[:], w2_q, z_q[0][:], z_q[1][:])
+            product(acc[:], w2_q, z_q[0], z_q[1])
             res = keep.tile([P, HALF], F32, name=f"res{u}")
             if u == 0:
                 nc.scalar.copy(res[:], acc[:])

from contextlib import ExitStack

import concourse.mybir as mybir
from concourse.masks import make_identity

K, T, S, V, H, N = 512, 1024, 512, 256, 512, 128
FLOPS = 2 * K * H * S + 2 * H * N * V

F32 = mybir.dt.float32
BF16 = mybir.dt.bfloat16
I32 = mybir.dt.int32
U32 = mybir.dt.uint32
U16 = mybir.dt.uint16
U8 = mybir.dt.uint8
FP8X4 = mybir.dt.float8_e4m3fn_x4
ALU = mybir.AluOpType
ACT = mybir.ActivationFunctionType

P = 128
PACK = 4
TILES = H // P
HALF = V // 2
Q = P // 2
WHOLE = slice(0, V)
HALVES = (slice(0, HALF), slice(HALF, V))


def tile_picked_ymorph_lap_p_kernel(
    tc, x_words, x_scales, w1, w2, el, offs, pos1, pos2, pos3, out
):
    nc = tc.nc
    with ExitStack() as ctx:
        keep = ctx.enter_context(tc.tile_pool(name="keep", bufs=1))
        psum = ctx.enter_context(tc.psum_pool(name="psum", bufs=1))

        offs_sb = keep.tile([P, S // 16], U16, name="offs_sb")
        pos_sb = [keep.tile([P, V // 16], U16, name=f"pos{d}") for d in range(3)]
        xw = keep.tile([P, T], U32, name="xw", align_bytes=64)
        xs = keep.tile([P, T], U8, name="xs", align_bytes=64)
        w1_first = [keep.tile([P, 2, H // 2], F32, name=f"w1_first{r}") for r in range(2)]
        w1_second = keep.tile([P, PACK, H // 2], F32, name="w1_second")
        el_sb = keep.tile([P, PACK], F32, name="el_sb")
        ident = keep.tile([P, P], F32, name="ident")

        nc.gpsimd.memset(xs[:].bitcast(I32), 0)
        nc.sync.dma_start(offs_sb[:], offs)
        nc.sync.dma_start(xw[:].bitcast(I32), x_words[0].rearrange("p n t -> p (n t)").bitcast(I32))
        for q in range(4):
            nc.sync.dma_start(
                xs[32 * q : 32 * q + 4, :].bitcast(I32), x_scales[0, 4 * q : 4 * q + 4, :].bitcast(I32)
            )
        w1_v = w1.rearrange("(p j) c -> p j c", j=PACK)
        for r in range(2):
            nc.sync.dma_start(w1_first[r][:], w1_v[:, 2 * r : 2 * r + 2, 0 : H // 2])
        nc.sync.dma_start(w1_second[:], w1_v[:, :, H // 2 : H])
        for d, pos in enumerate((pos1, pos2, pos3)):
            nc.sync.dma_start(pos_sb[d][:], pos)
        nc.sync.dma_start(el_sb[:], el.rearrange("(p t) o -> p (t o)", t=PACK))
        make_identity(nc, ident[:])

        el_half = keep.tile([P, 2], F32, name="el_half")

        xq_s = keep.tile([P, S], U8, name="xq_s", align_bytes=64)
        xq_w = keep.tile([P, S], U32, name="xq_w", align_bytes=64)
        nc.vector.tensor_copy(xq_w[:], xw[:].indirect(offs_sb[:]))
        nc.vector.tensor_copy(xq_s[:], xs[:].indirect(offs_sb[:]))

        def quantise(grouped, name):
            width = grouped.shape[1] // PACK
            codes = keep.tile([P, width], U32, name=name + "_codes", align_bytes=64)
            scales = keep.tile([P, width], U8, name=name + "_scales", align_bytes=64)
            nc.vector.quantize_mx(out=codes[:].bitcast(FP8X4), scales=scales[:], in_=grouped)
            return codes[:], scales[:]

        def product(acc, lhs, codes, scales):
            nc.tensor.matmul_mx(
                out=acc,
                lhsT=lhs[0].bitcast(FP8X4),
                lhsT_scale=lhs[1],
                rhs=codes.bitcast(FP8X4),
                rhs_scale=scales,
                start=True,
                stop=True,
            )

        first_cols = [raw[:].rearrange("p j (m t) -> p m t j", t=PACK) for raw in w1_first]
        second_cols = w1_second[:].rearrange("p j (m t) -> p m t j", t=PACK)
        w1_pair = [keep.tile([P, 2, Q, PACK], BF16, name=f"w1_pair{c}", align_bytes=64) for c in range(2)]
        w1_slot = keep.tile([P, 2, P, PACK], BF16, name="w1_slot", align_bytes=64)
        h = [keep.tile([P, S], F32, name=f"h{j}") for j in range(TILES)]

        h_lifted = [keep.tile([P, S], F32, name=f"h_lifted{e}") for e in range(2)]
        extremes = []

        for r in range(2):
            nc.scalar.copy(
                w1_pair[0][:, :, :, 2 * r : 2 * r + 2].rearrange("p e m j -> p m e j"), first_cols[r][:, :, 0:2, :]
            )
        w1_q = [quantise(w1_pair[0][:].rearrange("p e m j -> p (e m j)"), "w1_0")]
        for u in range(2):
            cols = slice(u * S // 2, (u + 1) * S // 2)
            acc = psum.tile([P, S // 2], F32, name=f"narrow{u}")
            product(acc[:], w1_q[0], xq_w[:, cols], xq_s[:, cols])
            nc.vector.tensor_copy(h[0][:, cols], acc[:])

        def hidden(j):
            if j == 1:
                nc.scalar.copy(w1_pair[1][:].rearrange("p e m j -> p m e j"), second_cols[:, :, 0:2, :])
                w1_q.append(quantise(w1_pair[1][:].rearrange("p e m j -> p (e m j)"), "w1_1"))
            if j == 2:
                nc.scalar.mul(el_half[:], el_sb[:, 2:4], 0.5)
                for r in range(2):
                    nc.scalar.copy(
                        w1_slot[:, :, 0:Q, 2 * r : 2 * r + 2].rearrange("p e m j -> p m e j"),
                        first_cols[r][:, :, 2:4, :],
                    )
                nc.scalar.copy(w1_slot[:, :, Q:P, :].rearrange("p e m j -> p m e j"), second_cols[:, :, 2:4, :])
                codes, scales = quantise(w1_slot[:].rearrange("p e m j -> p (e m j)"), "w1_2")
                for e in range(2):
                    w1_q.append((codes[:, e * P : (e + 1) * P], scales[:, e * P : (e + 1) * P]))
            acc = psum.tile([P, S], F32, name=f"h_acc{j}")
            product(acc[:], w1_q[j], xq_w[:], xq_s[:])
            nc.scalar.copy(h[j][:], acc[:])
            if j >= 2:
                lift = keep.tile([P, 1], F32, name=f"extremes{j - 2}")
                nc.scalar.mul(lift[:], el_sb[:, j : j + 1], 0.5)
                nc.scalar.activation(h_lifted[j - 2][:], acc[:], ACT.Identity, bias=lift[:])
                extremes.append(keep.tile([P, 2, 2, V], F32, name=f"extremes{j - 2}"))

        base = [keep.tile([P, V], F32, name=f"base{j}") for j in range(TILES)]
        da = [keep.tile([P, 2, V], F32, name=f"da{c}") for c in range(2)]
        db = [keep.tile([P, 2, V], F32, name=f"db{c}") for c in range(2)]
        zt = [psum.tile([P, 2, P], F32, name=f"zt{u}") for u in range(2)]
        z_bf = [keep.tile([P, HALF, PACK], BF16, name=f"z_bf{u}", align_bytes=64) for u in range(2)]

        def centre(j, cols):
            offsets = pos_sb[0][:, cols.start // 16 : cols.stop // 16]
            nc.vector.tensor_copy(base[j][:, cols], h[j][:].indirect(offsets))

        def neighbour(j, d, cols):
            window = h[j] if j < 2 else h_lifted[j - 2]
            offsets = pos_sb[d][:, cols.start // 16 : cols.stop // 16]
            dst = (da, db)[d - 1][j // 2][:, j % 2, cols]
            nc.vector.tensor_tensor(dst, window[:].indirect(offsets), base[j][:, cols], ALU.subtract)

        def extreme(j, n, cols):
            op = (ALU.max, ALU.min)[n]
            if j == 1:
                nc.vector.scalar_tensor_tensor(extremes[0][:, n, :, :], da[0][:], 0.0, db[0][:], op, op)
            else:
                e = j - 2
                nc.vector.scalar_tensor_tensor(
                    extremes[1][:, n, e, cols], da[1][:, e, cols], el_half[:, e : e + 1], db[1][:, e, cols], op, op
                )

        def turn(dst, term, start, stop):
            nc.tensor.matmul(dst, term, ident[:], start=start, stop=stop, is_transpose=True)

        def turn_tile():
            for n in range(2):
                for u in range(2):
                    for j in range(2):
                        term = extremes[0][:, n, j, HALVES[u]]
                        turn(zt[u][:, :, j * Q : (j + 1) * Q], term, False, j == 1 and n == 1)

        def turn_back():
            back = psum.tile([P, 2, HALF], F32, name="back")
            for u in range(2):
                zt_bf = keep.tile([P, P, 2], BF16, name=f"zt_bf{u}")
                nc.scalar.copy(zt_bf[:], zt[u][:].rearrange("v e p -> v p e"))
                nc.tensor.transpose(back[:, u, :], zt_bf[:].rearrange("v p e -> v (p e)").bitcast(F32), ident[:])
            for u in range(2):
                words = z_bf[u][:].rearrange("p v t -> p (v t)").bitcast(F32).rearrange("p (v w) -> p v w", w=2)
                nc.scalar.copy(words[:, :, 0], back[:, u, :])

        for j in range(2):
            for cols in HALVES:
                centre(j, cols)
            hidden(j + 1)
            neighbour(j, 1, HALVES[0])
            neighbour(j, 2, WHOLE)
            neighbour(j, 1, HALVES[1])
        for u in range(2):
            for e in range(2):
                turn(zt[u][:, e, :], el_sb[:, e : e + 1].to_broadcast([P, HALF]), e == 0, False)

        centre(2, WHOLE)
        hidden(3)
        extreme(1, 0, WHOLE)
        neighbour(2, 1, WHOLE)
        extreme(1, 1, WHOLE)
        neighbour(2, 2, WHOLE)
        w2_raw = keep.tile([P, PACK, N], F32, name="w1_first0")
        nc.sync.dma_start(w2_raw[:], w2.rearrange("(p j) n -> p j n", j=PACK))
        w2_bf = keep.tile([P, N, PACK], BF16, name="w2_bf", align_bytes=64)
        nc.scalar.copy(
            w2_bf[:].rearrange("p (c i) j -> p c j i", i=4),
            w2_raw[:].rearrange("p j (c i) -> p c j i", i=4),
        )
        w2_q = quantise(w2_bf[:].rearrange("p n j -> p (n j)"), "w2")
        turn_tile()
        turn_back()

        centre(3, WHOLE)
        extreme(2, 0, WHOLE)
        neighbour(3, 1, WHOLE)
        neighbour(3, 2, WHOLE)
        extreme(2, 1, WHOLE)
        extreme(3, 0, WHOLE)
        for cols in HALVES:
            extreme(3, 1, cols)

        for u, cols in enumerate(HALVES):
            nc.vector.tensor_tensor(
                z_bf[u][:, :, 2:4].rearrange("p (c i) t -> p c t i", i=4),
                extremes[1][:, 0, :, cols].rearrange("p t (c i) -> p c t i", i=4),
                extremes[1][:, 1, :, cols].rearrange("p t (c i) -> p c t i", i=4),
                ALU.add,
            )
        for u in range(2):
            cols = slice(u * HALF, (u + 1) * HALF)
            z_q = quantise(z_bf[u][:].rearrange("p v t -> p (v t)"), f"z{u}")
            acc = psum.tile([P, HALF], F32, name=f"narrow{u}")
            product(acc[:], w2_q, z_q[0], z_q[1])
            res = keep.tile([P, HALF], F32, name=f"res{u}")
            if u == 0:
                nc.scalar.copy(res[:], acc[:])
                nc.scalar.dma_start(out[:, cols], res[:])
            else:
                nc.vector.tensor_copy(res[:], acc[:])
                nc.sync.dma_start(out[:, cols], res[:])
